import numpy as np
import ml_dtypes


def mxq(x, axis, fmt="e4m3"):
    dtype, down = {"e4m3": (ml_dtypes.float8_e4m3fn, 7), "e5m2": (ml_dtypes.float8_e5m2, 14)}[fmt]
    v = np.moveaxis(np.asarray(x, np.float32).astype(ml_dtypes.bfloat16).astype(np.float64), axis, -1)
    blocks = v.reshape(v.shape[:-1] + (-1, 32))
    amax = np.abs(blocks).max(-1, keepdims=True)
    byte = np.maximum(np.where(amax > 0, np.frexp(amax)[1] - 1 + 127, 0) - down, 1)
    scale = np.exp2(byte - 127.0)
    codes = (blocks / scale).astype(np.float32).astype(dtype).astype(np.float64)
    return np.moveaxis((codes * scale).reshape(v.shape), -1, axis)


WIDE = False


def mx_kscale(k):
    if not WIDE:
        return np.ones(k)
    levels = np.array([10, -10, 5, -5, 0])
    if k % 512:
        return np.exp2(np.random.permutation(np.resize(levels, k // 32))).repeat(32)
    a = np.empty((k // 512, 16))
    for p in range(k // 512):
        a[p, :8] = np.random.permutation(np.resize(levels, 8))
        for g in range(8):
            far = levels[np.abs(levels - a[p, g]) >= 10]
            a[p, g + 8] = far[np.random.randint(len(far))]
    return np.exp2(a.ravel()).repeat(32)


def f64(x):
    return np.asarray(x).astype(np.float64)


def striped(idx):
    return np.tile(idx.reshape(-1, 16).T, (8, 1)).astype(np.uint16)


def unstriped(offs):
    return offs[:16].T.reshape(-1).astype(np.int64)


E2M1 = np.array([0.0, 0.5, 1.0, 1.5, 2.0, 3.0, 4.0, 6.0, -0.0, -0.5, -1.0, -1.5, -2.0, -3.0, -4.0, -6.0])


def pack_weight(w, fmt):
    k, n = w.shape
    w = f64(np.asarray(w, np.float32).astype(ml_dtypes.bfloat16)).reshape(k // 32, 32, n)
    amax = np.abs(w).max(1)
    if fmt == "e4m3":
        byte = np.frexp(amax)[1] - 1 + 127 - 7
    else:
        mant, ex = np.frexp(amax / 6.0)
        byte = np.where(mant > 0.5, ex, ex - 1) + 127
    byte = np.clip(np.where(amax > 0, byte, 1), 1, 254)
    scaled = (w * np.exp2(127.0 - byte)[:, None, :]).reshape(k, n).astype(np.float32)
    by_word = np.ascontiguousarray(scaled.reshape(k // 512, 128, 4, n).transpose(0, 1, 3, 2))
    if fmt == "e4m3":
        words = by_word.astype(ml_dtypes.float8_e4m3fn).view(np.uint8)
    else:
        c = by_word.astype(ml_dtypes.float4_e2m1fn).view(np.uint8) & 0xF
        words = (c[..., 0::2] | (c[..., 1::2] << 4)).reshape(k // 512, 128, 2 * n)
    return np.ascontiguousarray(words), np.ascontiguousarray(byte.astype(np.uint8).reshape(k // 512, 16, n))


def unpack_weight(words, scales, fmt):
    g, _, n = scales.shape
    words = np.ascontiguousarray(words).reshape(g, 128, n, -1)
    if fmt == "e4m3":
        vals = words.view(ml_dtypes.float8_e4m3fn).astype(np.float64)
    else:
        nib = np.empty((g, 128, n, 4), np.uint8)
        nib[..., 0::2] = words & 0xF
        nib[..., 1::2] = words >> 4
        vals = E2M1[nib]
    vals = vals * np.repeat(np.exp2(scales.astype(np.float64) - 127.0), 8, axis=1)[..., None]
    return vals.transpose(0, 1, 3, 2).reshape(g * 512, n)


def gelu(v):
    return 0.5 * v * (1.0 + np.tanh(np.sqrt(2.0 / np.pi) * (v + 0.044715 * v**3)))


K, KA, T, H, S, T2, P, S2, T3 = 1536, 1024, 4096, 512, 1024, 2048, 512, 1024, 2048


def setup_inputs():
    n = np.random.standard_normal
    s = mx_kscale(K)[:, None]
    u = mx_kscale(H)[:, None]
    tab_words, tab_scales = pack_weight(n((K, T)) * s, "e4m3")
    tab2_words, tab2_scales = pack_weight(n((H, T3)) / np.sqrt(H) / u, "e4m3")
    w4_words, w4_scales = pack_weight(1.4 * n((K - KA, H)) / np.sqrt(K) / s[KA:], "e2m1")
    return {
        "tab_words": tab_words, "tab_scales": tab_scales,
        "tab2_words": tab2_words, "tab2_scales": tab2_scales,
        "w1": (1.4 * n((KA, H)) / np.sqrt(K) / s[:KA]).astype(np.float32),
        "w4_words": w4_words, "w4_scales": w4_scales,
        "shot": np.exp(0.5 * n((H, S))).astype(np.float32),
        "b1": (0.6 * n(H)).astype(np.float32),
        "gain": (1.2 * np.exp(0.3 * n(H)) * u[:, 0]).astype(np.float32),
        "page0": (n((H, T2)) * u).astype(np.float32),
        "wgs": np.exp(0.3 * n((128, S))).astype(np.float32),
        "ca": np.exp(0.4 * n(S2)).astype(np.float32),
        "cb": (0.7 * n(S2)).astype(np.float32),
        "offs": striped(np.random.permutation(T)[:S]),
        "offs2": striped(np.random.permutation(T3)[:S2]),
        "offs3": striped(np.random.permutation(T2)[:S]),
        "offs4": striped(np.random.permutation(T2)[:P]),
    }


def reference(tab_words, tab_scales, tab2_words, tab2_scales, w1, w4_words, w4_scales,
              shot, b1, gain, page0, wgs, ca, cb, offs, offs2, offs3, offs4):
    v = unpack_weight(tab_words, tab_scales, "e4m3")[:, unstriped(offs)]
    v2 = unpack_weight(tab2_words, tab2_scales, "e4m3")[:, unstriped(offs2)]
    w4 = unpack_weight(w4_words, w4_scales, "e2m1")
    f = mxq(f64(w1), 0, "e4m3").T @ v[:KA] + w4.T @ v[KA:]
    h = f64(gain)[:, None] * np.tanh(f * f64(shot) + f64(b1)[:, None])
    page = f64(page0).copy()
    page[:, unstriped(offs3)] = np.tile(f64(wgs), (H // 128, 1)) * h
    x = np.abs(page[:, unstriped(offs4)])
    e = v2.T @ mxq(x, 0, "e4m3")
    return e * f64(ca)[:, None] + f64(cb)[:, None]

@@ -1,0 +1,236 @@
+from contextlib import ExitStack
+
+import concourse.mybir as mybir
+
+K, KA, T, H, S, T2, PJ, S2, T3 = 1536, 1024, 4096, 512, 1024, 2048, 512, 1024, 2048
+FLOPS = 2 * K * H * S + 2 * H * S2 * PJ
+
+F32 = mybir.dt.float32
+BF16 = mybir.dt.bfloat16
+I32 = mybir.dt.int32
+U32 = mybir.dt.uint32
+U16 = mybir.dt.uint16
+U8 = mybir.dt.uint8
+FP8X4 = mybir.dt.float8_e4m3fn_x4
+FP4X4 = mybir.dt.float4_e2m1fn_x4
+ACT = mybir.ActivationFunctionType
+MULT = mybir.AluOpType.mult
+ADD = mybir.AluOpType.add
+
+P = 128
+PACK = 4
+BANK = 512
+TAB_PLANE = (4, 8, 0)
+TAB2_PLANE = 12
+
+
+def tile_list_footage_clip_storyboard_kernel(
+    tc, tab_words, tab_scales, tab2_words, tab2_scales, w1, w4_words, w4_scales,
+    shot, b1, gain, page0, wgs, ca, cb, offs, offs2, offs3, offs4, out,
+):
+    nc = tc.nc
+    with ExitStack() as ctx:
+        keep = ctx.enter_context(tc.tile_pool(name="keep", bufs=1))
+        psum = ctx.enter_context(tc.psum_pool(name="psum", bufs=8))
+
+        def sb(name, width, dtype, slot=None):
+            return keep.tile([P, width], dtype, name=name, tag=slot or name, align_bytes=64)
+
+        def words(table, a):
+            return table[a].rearrange("p t i -> p (t i)").bitcast(I32)
+
+        shot_rows = shot.rearrange("(p t) j -> p t j", t=PACK)
+        page_rows = page0.rearrange("(p t) j -> p t j", t=PACK)
+        wgs_rows = wgs.rearrange("(q t) j -> q t j", t=PACK)
+
+        def load_wgs(dst, first, t, lo, hi):
+            for g in (0, 2, 1, 3):
+                nc.sync.dma_start(out=dst[32 * g : 32 * g + 32, first : first + hi - lo], in_=wgs_rows[:, t, lo:hi])
+
+        def load_page(t, slot):
+            tile = sb("page%d" % t, T2, F32, slot)
+            nc.sync.dma_start(out=tile[:], in_=page_rows[:, t, :])
+            return tile
+
+        list1 = keep.tile([P, S // 16], U16, name="list1")
+        list2 = keep.tile([P, S2 // 16], U16, name="list2")
+        list3 = keep.tile([P, S // 16], U16, name="list3")
+        list4 = keep.tile([P, PJ // 16], U16, name="list4")
+
+        tab_s = sb("tab_s", T, U8)
+        tab2_s = sb("tab2_s", T3, U8)
+        w4_raw_s = sb("w4_raw_s", H, U8)
+        nc.vector.memset(tab_s[:].bitcast(I32), 0)
+        nc.gpsimd.memset(w4_raw_s[:].bitcast(I32), 0)
+        nc.gpsimd.memset(tab2_s[:].bitcast(I32), 0)
+
+        w4_raw = sb("w4_raw", 2 * H, U8, "B")
+        tab_w0 = sb("tab_w0", T, I32, "A")
+        w1_raw = [sb("w1_raw0", PACK * H, F32, "C"), sb("w1_raw1", PACK * H, F32, "D")]
+        b1_sb = sb("b1_sb", PACK, F32)
+        gain_sb = sb("gain_sb", PACK, F32)
+        nc.sync.dma_start(out=w4_raw[:].bitcast(I32), in_=w4_words[0].bitcast(I32))
+        nc.sync.dma_start(list1[:], offs)
+        nc.sync.dma_start(out=tab_w0[:], in_=words(tab_words, 0))
+        nc.sync.dma_start(list2[:], offs2)
+        nc.sync.dma_start(list3[:], offs3)
+        nc.sync.dma_start(list4[:], offs4)
+        for a in range(2):
+            nc.sync.dma_start(out=w1_raw[a][:],
+                              in_=w1[512 * a : 512 * (a + 1), :].rearrange("(p j) c -> p (j c)", j=PACK))
+        nc.sync.dma_start(out=b1_sb[:], in_=b1.rearrange("(p t) -> p t", t=PACK))
+        nc.sync.dma_start(out=gain_sb[:], in_=gain.rearrange("(p t) -> p t", t=PACK))
+        tab_s_words = tab_scales.bitcast(I32)
+        for q in (0, 2, 1, 3):
+            nc.gpsimd.dma_start(out=tab_s[32 * q + 4 : 32 * q + 12, :].bitcast(I32),
+                              in_=tab_s_words[0:2, 4 * q : 4 * q + 4, :])
+            nc.sync.dma_start(out=tab_s[32 * q : 32 * q + 4, :].bitcast(I32),
+                              in_=tab_s_words[2, 4 * q : 4 * q + 4, :])
+        for q in range(4):
+            nc.gpsimd.dma_start(out=w4_raw_s[32 * q : 32 * q + 4, :].bitcast(I32),
+                                in_=w4_scales.bitcast(I32)[0, 4 * q : 4 * q + 4, :])
+        for q in range(4):
+            row = 32 * q + TAB2_PLANE
+            nc.gpsimd.dma_start(out=tab2_s[row : row + 4, :].bitcast(I32),
+                                in_=tab2_scales.bitcast(I32)[0, 4 * q : 4 * q + 4, :])
+
+        w4_codes = sb("w4_codes", 2 * H, U8)
+        nc.vector.tensor_copy(out=w4_codes[:].rearrange("p (t m b) -> p m t b", t=PACK, b=2),
+                              in_=w4_raw[:].rearrange("p (m t b) -> p m t b", t=PACK, b=2))
+        tab_w1 = sb("tab_w1", T, I32, "B")
+        nc.sync.dma_start(out=tab_w1[:], in_=words(tab_words, 1))
+
+        v_w = [sb("v_w%d" % a, S, U32) for a in range(2)]
+        nc.vector.tensor_copy(out=v_w[0][:], in_=tab_w0[:].bitcast(U32).indirect(list1[:]))
+        tab_w2 = sb("tab_w2", T, I32, "A")
+        nc.sync.dma_start(out=tab_w2[:], in_=words(tab_words, 2))
+
+        w1_codes, w1_scales = [], []
+        for a in range(2):
+            rounded = sb("w1_bf%d" % a, PACK * H, BF16, "EF"[a])
+            nc.scalar.copy(out=rounded[:].rearrange("p (t m j) -> p m t j", t=PACK, j=PACK),
+                           in_=w1_raw[a][:].rearrange("p (j m t) -> p m t j", j=PACK, t=PACK))
+            codes = sb("w1_codes%d" % a, H, U32)
+            scales = sb("w1_scales%d" % a, H, U8)
+            nc.vector.quantize_mx(out=codes[:].bitcast(FP8X4), scales=scales[:], in_=rounded[:])
+            w1_codes.append(codes)
+            w1_scales.append(scales)
+
+        shot0 = sb("shot0", S, F32, "C")
+        nc.sync.dma_start(out=shot0[:], in_=shot_rows[:, 0, :])
+        wgs00 = sb("wgs00", BANK, F32, "E")
+        load_wgs(wgs00, 0, 0, 0, BANK)
+        page = [load_page(0, "D")]
+
+        v_s = sb("v_s", S, U8)
+        nc.vector.tensor_copy(out=v_s[:], in_=tab_s[:].indirect(list1[:]))
+        w4_s = sb("w4_s", H, U8)
+        nc.vector.tensor_copy(out=w4_s[:].rearrange("p (t m) -> p m t", t=PACK),
+                              in_=w4_raw_s[:].rearrange("p (m t) -> p m t", t=PACK))
+        nc.vector.tensor_copy(out=v_w[1][:], in_=tab_w1[:].bitcast(U32).indirect(list1[:]))
+
+        later = sb("later", 4 * S, F32, "B")
+        nc.sync.dma_start(out=later[:, 0:S], in_=shot_rows[:, 1, :])
+        load_wgs(later, 3 * S, 0, BANK, S)
+        nc.sync.dma_start(out=later[:, S : 2 * S], in_=shot_rows[:, 2, :])
+        nc.sync.dma_start(out=later[:, 2 * S : 3 * S], in_=shot_rows[:, 3, :])
+        shot_sb = [shot0[:], later[:, 0:S], later[:, S : 2 * S], later[:, 2 * S : 3 * S]]
+
+        v_w2 = [sb("v_w2_%d" % h, BANK, U32) for h in range(2)]
+        for h in range(2):
+            nc.vector.tensor_copy(out=v_w2[h][:],
+                                  in_=tab_w2[:].bitcast(U32).indirect(list1[:, 32 * h : 32 * (h + 1)]))
+        v2_s = sb("v2_s", S2, U8)
+        nc.vector.tensor_copy(out=v2_s[:], in_=tab2_s[:].indirect(list2[:]))
+
+        wgs12 = sb("wgs12", 2 * S, F32, "A")
+        load_wgs(wgs12, 0, 1, 0, S)
+
+        f_acc = [[psum.tile([P, BANK], F32, name="acc") for h in range(2)] for t in range(PACK)]
+        for t in range(PACK):
+            for h in range(2):
+                for a in range(3):
+                    cols = slice(h * BANK, (h + 1) * BANK)
+                    if a < 2:
+                        lhs = w1_codes[a][:, P * t : P * (t + 1)].bitcast(FP8X4)
+                        lhs_s = w1_scales[a][:, P * t : P * (t + 1)]
+                        rhs = v_w[a][:, cols]
+                    else:
+                        lhs = w4_codes[:, 2 * P * t : 2 * P * (t + 1)].bitcast(FP4X4)
+                        lhs_s = w4_s[:, P * t : P * (t + 1)]
+                        rhs = v_w2[h][:]
+                    nc.tensor.matmul_mx(out=f_acc[t][h][:], lhsT=lhs, lhsT_scale=lhs_s,
+                                        rhs=rhs.bitcast(FP8X4), rhs_scale=v_s[TAB_PLANE[a] : P, cols],
+                                        start=(a == 0), stop=(a == 2))
+
+        def times_shot(dst, t, h):
+            nc.vector.tensor_tensor(out=dst, in0=f_acc[t][h][:],
+                                    in1=shot_sb[t][:, h * BANK : (h + 1) * BANK], op=MULT)
+
+        def tanh_gain(z, t):
+            nc.scalar.activation(out=z, in_=z, func=ACT.Tanh, bias=b1_sb[:, t : t + 1])
+            nc.scalar.activation(out=z, in_=z, func=ACT.Copy, scale=gain_sb[:, t : t + 1])
+
+        x_bf = sb("x_bf", PACK * PJ, BF16)
+        x_slots = x_bf[:].rearrange("p (j t) -> p t j", t=PACK)
+
+        def pick(t):
+            picked = sb("picked%d" % t, PJ, F32)
+            nc.vector.tensor_copy(out=picked[:], in_=page[t][:].indirect(list4[:]))
+            nc.scalar.activation(out=x_slots[:, t, :], in_=picked[:], func=ACT.Abs)
+
+        z0 = [sb("z0_0", BANK, F32, "G"), sb("z0_1", BANK, F32, "H")]
+        for h in range(2):
+            times_shot(z0[h][:], 0, h)
+            tanh_gain(z0[h][:], 0)
+        page.append(load_page(1, "C"))
+        load_wgs(wgs12, S, 2, 0, S)
+        nc.vector.tensor_tensor(out=page[0][:].indirect(list3[:, 0:32]), in0=z0[0][:], in1=wgs00[:], op=MULT)
+        page.append(load_page(2, "G"))
+        wgs3 = sb("wgs3", S + 16, F32, "E")
+        load_wgs(wgs3, 0, 3, 0, S)
+        z = [None]
+        for t in range(1, PACK):
+            z.append(sb("z%d" % t, S, F32, "IJK"[t - 1]))
+            for h in range(2):
+                times_shot(z[t][:, h * BANK : (h + 1) * BANK], t, h)
+            tanh_gain(z[t][:], t)
+            if t == 1:
+                nc.vector.tensor_tensor(out=page[0][:].indirect(list3[:, 32:64]), in0=z0[1][:],
+                                        in1=later[:, 3 * S : 3 * S + BANK], op=MULT)
+                page.append(load_page(3, "H"))
+                pick(0)
+        wgs_sb = [None, wgs12[:, 0:S], wgs12[:, S : 2 * S], wgs3[:, 0:S]]
+        for t in range(1, PACK):
+            nc.vector.tensor_tensor(out=page[t][:].indirect(list3[:]), in0=z[t][:], in1=wgs_sb[t], op=MULT)
+            if t == 1:
+                tab2_w = sb("tab2_w", T3, I32, "I")
+                nc.sync.dma_start(out=tab2_w[:], in_=words(tab2_words, 0))
+                ca_sb = wgs3[:, S : S + 8]
+                cb_sb = wgs3[:, S + 8 : S + 16]
+                with nc.allow_non_contiguous_dma(reason="one value of ca and cb for each output row"):
+                    nc.sync.dma_start(out=ca_sb, in_=ca.rearrange("(c p) -> p c", p=P))
+                    nc.sync.dma_start(out=cb_sb, in_=cb.rearrange("(c p) -> p c", p=P))
+            pick(t)
+
+        v2_w = [sb("v2_w%d" % h, BANK, U32) for h in range(2)]
+        x_codes = sb("x_codes", PJ, U32)
+        x_scales = sb("x_scales", PJ, U8)
+        nc.vector.tensor_copy(out=v2_w[0][:], in_=tab2_w[:].bitcast(U32).indirect(list2[:, 0:32]))
+        nc.vector.quantize_mx(out=x_codes[:].bitcast(FP8X4), scales=x_scales[:], in_=x_bf[:])
+        nc.vector.tensor_copy(out=v2_w[1][:], in_=tab2_w[:].bitcast(U32).indirect(list2[:, 32:64]))
+        for c in range(S2 // P):
+            e_acc = psum.tile([P, BANK], F32, name="acc")
+            nc.tensor.matmul_mx(out=e_acc[:],
+                                lhsT=v2_w[c // 4][:, P * (c % 4) : P * (c % 4 + 1)].bitcast(FP8X4),
+                                lhsT_scale=v2_s[TAB2_PLANE:P, P * c : P * (c + 1)],
+                                rhs=x_codes[:].bitcast(FP8X4), rhs_scale=x_scales[:],
+                                start=True, stop=True)
+            res = sb("res%d" % c, PJ, F32)
+            if c in (3, 5, 7):
+                nc.vector.tensor_scalar(out=res[:], in0=e_acc[:], scalar1=ca_sb[:, c : c + 1],
+                                        scalar2=cb_sb[:, c : c + 1], op0=MULT, op1=ADD)
+            else:
+                nc.scalar.activation(out=res[:], in_=e_acc[:], func=ACT.Identity,
+                                     scale=ca_sb[:, c : c + 1], bias=cb_sb[:, c : c + 1])
+            nc.sync.dma_start(out=out[P * c : P * (c + 1), :], in_=res[:])

@@ -22,6 +22,7 @@ PACK = 4
 BANK = 512
 TAB_PLANE = (4, 8, 0)
 TAB2_PLANE = 12
+QUADS = (0, 2, 1, 3)
 
 
 def tile_list_footage_clip_storyboard_kernel(
@@ -36,6 +37,26 @@ def tile_list_footage_clip_storyboard_kernel(
         def sb(name, width, dtype, slot=None):
             return keep.tile([P, width], dtype, name=name, tag=slot or name, align_bytes=64)
 
+        list1 = keep.tile([P, S // 16], U16, name="list1")
+        list2 = keep.tile([P, S2 // 16], U16, name="list2")
+        list3 = keep.tile([P, S // 16], U16, name="list3")
+        list4 = keep.tile([P, PJ // 16], U16, name="list4")
+
+        tab_w = [sb("tab_w%d" % a, T, I32) for a in range(3)]
+        tab_s = sb("tab_s", T, U8)
+        tab2_s = sb("tab2_s", T3, U8)
+        w1_raw = [sb("w1_raw%d" % a, PACK * H, F32) for a in range(2)]
+        w4_raw = sb("w4_raw", 2 * H, U8)
+        w4_raw_s = sb("w4_raw_s", H, U8)
+        b1_sb = sb("b1_sb", PACK, F32)
+        gain_sb = sb("gain_sb", PACK, F32)
+        ca_sb = sb("ca_sb", S2 // P, F32)
+        cb_sb = sb("cb_sb", S2 // P, F32)
+        shot_sb = [sb("shot%d" % t, S, F32) for t in range(PACK)]
+        wgs_sb = [sb("wgs%d" % t, S, F32) for t in range(PACK)]
+        page = [sb("page%d" % t, T2, F32) for t in range(PACK)]
+        tab2_w = sb("tab2_w", T3, I32)
+
         def words(table, a):
             return table[a].rearrange("p t i -> p (t i)").bitcast(I32)
 
@@ -43,108 +64,85 @@ def tile_list_footage_clip_storyboard_kernel(
         page_rows = page0.rearrange("(p t) j -> p t j", t=PACK)
         wgs_rows = wgs.rearrange("(q t) j -> q t j", t=PACK)
 
-        def load_wgs(dst, first, t, lo, hi):
-            for g in (0, 2, 1, 3):
-                nc.sync.dma_start(out=dst[32 * g : 32 * g + 32, first : first + hi - lo], in_=wgs_rows[:, t, lo:hi])
+        def wgs_loads(t, lo, hi):
+            return [(wgs_sb[t][32 * g : 32 * g + 32, lo:hi], wgs_rows[:, t, lo:hi]) for g in QUADS]
 
-        def load_page(t, slot):
-            tile = sb("page%d" % t, T2, F32, slot)
-            nc.sync.dma_start(out=tile[:], in_=page_rows[:, t, :])
-            return tile
+        def scale_loads(tile, first, scales, a):
+            return [(tile[32 * q + first : 32 * q + first + 4, :].bitcast(I32),
+                     scales.bitcast(I32)[a, 4 * q : 4 * q + 4, :]) for q in QUADS]
 
-        list1 = keep.tile([P, S // 16], U16, name="list1")
-        list2 = keep.tile([P, S2 // 16], U16, name="list2")
-        list3 = keep.tile([P, S // 16], U16, name="list3")
-        list4 = keep.tile([P, PJ // 16], U16, name="list4")
-
-        tab_s = sb("tab_s", T, U8)
-        tab2_s = sb("tab2_s", T3, U8)
-        w4_raw_s = sb("w4_raw_s", H, U8)
         nc.vector.memset(tab_s[:].bitcast(I32), 0)
-        nc.gpsimd.memset(w4_raw_s[:].bitcast(I32), 0)
         nc.gpsimd.memset(tab2_s[:].bitcast(I32), 0)
+        nc.gpsimd.memset(w4_raw_s[:].bitcast(I32), 0)
 
-        w4_raw = sb("w4_raw", 2 * H, U8, "B")
-        tab_w0 = sb("tab_w0", T, I32, "A")
-        w1_raw = [sb("w1_raw0", PACK * H, F32, "C"), sb("w1_raw1", PACK * H, F32, "D")]
-        b1_sb = sb("b1_sb", PACK, F32)
-        gain_sb = sb("gain_sb", PACK, F32)
-        nc.sync.dma_start(out=w4_raw[:].bitcast(I32), in_=w4_words[0].bitcast(I32))
-        nc.sync.dma_start(list1[:], offs)
-        nc.sync.dma_start(out=tab_w0[:], in_=words(tab_words, 0))
-        nc.sync.dma_start(list2[:], offs2)
-        nc.sync.dma_start(list3[:], offs3)
-        nc.sync.dma_start(list4[:], offs4)
-        for a in range(2):
-            nc.sync.dma_start(out=w1_raw[a][:],
-                              in_=w1[512 * a : 512 * (a + 1), :].rearrange("(p j) c -> p (j c)", j=PACK))
-        nc.sync.dma_start(out=b1_sb[:], in_=b1.rearrange("(p t) -> p t", t=PACK))
-        nc.sync.dma_start(out=gain_sb[:], in_=gain.rearrange("(p t) -> p t", t=PACK))
-        tab_s_words = tab_scales.bitcast(I32)
-        for q in (0, 2, 1, 3):
-            nc.gpsimd.dma_start(out=tab_s[32 * q + 4 : 32 * q + 12, :].bitcast(I32),
-                              in_=tab_s_words[0:2, 4 * q : 4 * q + 4, :])
-            nc.sync.dma_start(out=tab_s[32 * q : 32 * q + 4, :].bitcast(I32),
-                              in_=tab_s_words[2, 4 * q : 4 * q + 4, :])
-        for q in range(4):
-            nc.gpsimd.dma_start(out=w4_raw_s[32 * q : 32 * q + 4, :].bitcast(I32),
-                                in_=w4_scales.bitcast(I32)[0, 4 * q : 4 * q + 4, :])
-        for q in range(4):
-            row = 32 * q + TAB2_PLANE
-            nc.gpsimd.dma_start(out=tab2_s[row : row + 4, :].bitcast(I32),
-                                in_=tab2_scales.bitcast(I32)[0, 4 * q : 4 * q + 4, :])
+        def tab_half(a, u):
+            cols = slice(u * T // 2, (u + 1) * T // 2)
+            return (tab_w[a][:, cols], words(tab_words, a)[:, cols])
 
-        w4_codes = sb("w4_codes", 2 * H, U8)
-        nc.vector.tensor_copy(out=w4_codes[:].rearrange("p (t m b) -> p m t b", t=PACK, b=2),
-                              in_=w4_raw[:].rearrange("p (m t b) -> p m t b", t=PACK, b=2))
-        tab_w1 = sb("tab_w1", T, I32, "B")
-        nc.sync.dma_start(out=tab_w1[:], in_=words(tab_words, 1))
+        def w1_rows(a):
+            return (w1_raw[a][:], w1[512 * a : 512 * (a + 1), :].rearrange("(p j) c -> p (j c)", j=PACK))
+
+        tab_s_loads = []
+        for a in range(3):
+            tab_s_loads.extend(scale_loads(tab_s, TAB_PLANE[a], tab_scales, a))
+        loads = [tab_half(0, 0), (list1[:], offs), (w4_raw[:].bitcast(I32), w4_words[0].bitcast(I32)), tab_half(0, 1),
+                 (list2[:], offs2), (list3[:], offs3),
+                 (b1_sb[:], b1.rearrange("(p t) -> p t", t=PACK)),
+                 (gain_sb[:], gain.rearrange("(p t) -> p t", t=PACK)), w1_rows(0)]
+        loads.extend(scale_loads(tab2_s, TAB2_PLANE, tab2_scales, 0))
+        loads.extend(tab_s_loads[:2])
+        loads.append(w1_rows(1))
+        loads.extend(tab_s_loads[2:8])
+        loads.append(tab_half(1, 0))
+        loads.extend(tab_s_loads[8:])
+        loads.extend([tab_half(1, 1), tab_half(2, 0)])
+        loads.extend(scale_loads(w4_raw_s, 0, w4_scales, 0))
+        loads.extend([tab_half(2, 1), (shot_sb[0][:], shot_rows[:, 0, :]), (shot_sb[1][:], shot_rows[:, 1, :])])
+        loads.extend(wgs_loads(0, 0, BANK))
+        loads.append((page[0][:], page_rows[:, 0, :]))
+        loads.extend(wgs_loads(0, BANK, S))
+        loads.append((list4[:], offs4))
+        for t in range(1, PACK):
+            if t + 1 < PACK:
+                loads.append((shot_sb[t + 1][:], shot_rows[:, t + 1, :]))
+            else:
+                loads.append((tab2_w[:], words(tab2_words, 0)))
+            loads.extend(wgs_loads(t, 0, S))
+            loads.append((page[t][:], page_rows[:, t, :]))
+        for pair in loads:
+            nc.sync.dma_start(*pair)
+        with nc.allow_non_contiguous_dma(reason="one value of ca and cb for each output row"):
+            nc.sync.dma_start(out=ca_sb[:], in_=ca.rearrange("(c p) -> p c", p=P))
+            nc.sync.dma_start(out=cb_sb[:], in_=cb.rearrange("(c p) -> p c", p=P))
 
         v_w = [sb("v_w%d" % a, S, U32) for a in range(2)]
-        nc.vector.tensor_copy(out=v_w[0][:], in_=tab_w0[:].bitcast(U32).indirect(list1[:]))
-        tab_w2 = sb("tab_w2", T, I32, "A")
-        nc.sync.dma_start(out=tab_w2[:], in_=words(tab_words, 2))
+        v_w2 = [sb("v_w2_%d" % h, BANK, U32) for h in range(2)]
+        v_s = sb("v_s", S, U8)
+        v2_s = sb("v2_s", S2, U8)
+        w4_codes = sb("w4_codes", 2 * H, U8)
+        w4_s = sb("w4_s", H, U8)
+        w1_codes = [sb("w1_codes%d" % a, H, U32) for a in range(2)]
+        w1_scales = [sb("w1_scales%d" % a, H, U8) for a in range(2)]
 
-        w1_codes, w1_scales = [], []
-        for a in range(2):
-            rounded = sb("w1_bf%d" % a, PACK * H, BF16, "EF"[a])
+        def quantise_w1(a):
+            rounded = sb("w1_bf%d" % a, PACK * H, BF16)
             nc.scalar.copy(out=rounded[:].rearrange("p (t m j) -> p m t j", t=PACK, j=PACK),
                            in_=w1_raw[a][:].rearrange("p (j m t) -> p m t j", j=PACK, t=PACK))
-            codes = sb("w1_codes%d" % a, H, U32)
-            scales = sb("w1_scales%d" % a, H, U8)
-            nc.vector.quantize_mx(out=codes[:].bitcast(FP8X4), scales=scales[:], in_=rounded[:])
-            w1_codes.append(codes)
-            w1_scales.append(scales)
+            nc.vector.quantize_mx(out=w1_codes[a][:].bitcast(FP8X4), scales=w1_scales[a][:], in_=rounded[:])
 
-        shot0 = sb("shot0", S, F32, "C")
-        nc.sync.dma_start(out=shot0[:], in_=shot_rows[:, 0, :])
-        wgs00 = sb("wgs00", BANK, F32, "E")
-        load_wgs(wgs00, 0, 0, 0, BANK)
-        page = [load_page(0, "D")]
-
-        v_s = sb("v_s", S, U8)
+        nc.vector.tensor_copy(out=v_w[0][:], in_=tab_w[0][:].bitcast(U32).indirect(list1[:]))
+        quantise_w1(0)
         nc.vector.tensor_copy(out=v_s[:], in_=tab_s[:].indirect(list1[:]))
-        w4_s = sb("w4_s", H, U8)
-        nc.vector.tensor_copy(out=w4_s[:].rearrange("p (t m) -> p m t", t=PACK),
-                              in_=w4_raw_s[:].rearrange("p (m t) -> p m t", t=PACK))
-        nc.vector.tensor_copy(out=v_w[1][:], in_=tab_w1[:].bitcast(U32).indirect(list1[:]))
-
-        later = sb("later", 4 * S, F32, "B")
-        nc.sync.dma_start(out=later[:, 0:S], in_=shot_rows[:, 1, :])
-        load_wgs(later, 3 * S, 0, BANK, S)
-        nc.sync.dma_start(out=later[:, S : 2 * S], in_=shot_rows[:, 2, :])
-        nc.sync.dma_start(out=later[:, 2 * S : 3 * S], in_=shot_rows[:, 3, :])
-        shot_sb = [shot0[:], later[:, 0:S], later[:, S : 2 * S], later[:, 2 * S : 3 * S]]
-
-        v_w2 = [sb("v_w2_%d" % h, BANK, U32) for h in range(2)]
+        quantise_w1(1)
+        nc.vector.tensor_copy(out=v_w[1][:], in_=tab_w[1][:].bitcast(U32).indirect(list1[:]))
         for h in range(2):
             nc.vector.tensor_copy(out=v_w2[h][:],
-                                  in_=tab_w2[:].bitcast(U32).indirect(list1[:, 32 * h : 32 * (h + 1)]))
-        v2_s = sb("v2_s", S2, U8)
+                                  in_=tab_w[2][:].bitcast(U32).indirect(list1[:, 32 * h : 32 * (h + 1)]))
+        nc.vector.tensor_copy(out=w4_codes[:].rearrange("p (t m b) -> p m t b", t=PACK, b=2),
+                              in_=w4_raw[:].rearrange("p (m t b) -> p m t b", t=PACK, b=2))
+        nc.vector.tensor_copy(out=w4_s[:].rearrange("p (t m) -> p m t", t=PACK),
+                              in_=w4_raw_s[:].rearrange("p (m t) -> p m t", t=PACK))
         nc.vector.tensor_copy(out=v2_s[:], in_=tab2_s[:].indirect(list2[:]))
-
-        wgs12 = sb("wgs12", 2 * S, F32, "A")
-        load_wgs(wgs12, 0, 1, 0, S)
 
         f_acc = [[psum.tile([P, BANK], F32, name="acc") for h in range(2)] for t in range(PACK)]
         for t in range(PACK):
@@ -163,74 +161,88 @@ def tile_list_footage_clip_storyboard_kernel(
                                         rhs=rhs.bitcast(FP8X4), rhs_scale=v_s[TAB_PLANE[a] : P, cols],
                                         start=(a == 0), stop=(a == 2))
 
-        def times_shot(dst, t, h):
-            nc.vector.tensor_tensor(out=dst, in0=f_acc[t][h][:],
-                                    in1=shot_sb[t][:, h * BANK : (h + 1) * BANK], op=MULT)
+        HALF = PJ // 2
+        x_bf = [sb("x_bf%d" % u, PACK * HALF, BF16) for u in range(2)]
+        x_slots = [x_bf[u][:].rearrange("p (j t) -> p t j", t=PACK) for u in range(2)]
+        z = {}
 
-        def tanh_gain(z, t):
-            nc.scalar.activation(out=z, in_=z, func=ACT.Tanh, bias=b1_sb[:, t : t + 1])
-            nc.scalar.activation(out=z, in_=z, func=ACT.Copy, scale=gain_sb[:, t : t + 1])
+        def times_shot(t):
+            z[t] = sb("z%d" % t, S, F32, "z%d" % (t % 2))
+            for h in range(2):
+                cols = slice(h * BANK, (h + 1) * BANK)
+                nc.vector.tensor_tensor(out=z[t][:, cols], in0=f_acc[t][h][:], in1=shot_sb[t][:, cols], op=MULT)
 
-        x_bf = sb("x_bf", PACK * PJ, BF16)
-        x_slots = x_bf[:].rearrange("p (j t) -> p t j", t=PACK)
+        def tanh_gain(t, cols):
+            nc.scalar.activation(out=z[t][:, cols], in_=z[t][:, cols], func=ACT.Tanh, bias=b1_sb[:, t : t + 1])
+            nc.scalar.activation(out=z[t][:, cols], in_=z[t][:, cols], func=ACT.Copy, scale=gain_sb[:, t : t + 1])
+
+        def put(t, lo, hi):
+            nc.vector.tensor_tensor(out=page[t][:].indirect(list3[:, lo // 16 : hi // 16]),
+                                    in0=z[t][:, lo:hi], in1=wgs_sb[t][:, lo:hi], op=MULT)
+
+        picked = [sb("picked%d" % t, PJ, F32) for t in range(PACK)]
 
         def pick(t):
-            picked = sb("picked%d" % t, PJ, F32)
-            nc.vector.tensor_copy(out=picked[:], in_=page[t][:].indirect(list4[:]))
-            nc.scalar.activation(out=x_slots[:, t, :], in_=picked[:], func=ACT.Abs)
+            nc.vector.tensor_copy(out=picked[t][:], in_=page[t][:].indirect(list4[:]))
+            for u in range(2):
+                nc.scalar.activation(out=x_slots[u][:, t, :], in_=picked[t][:, u * HALF : (u + 1) * HALF], func=ACT.Abs)
 
-        z0 = [sb("z0_0", BANK, F32, "G"), sb("z0_1", BANK, F32, "H")]
+        times_shot(0)
         for h in range(2):
-            times_shot(z0[h][:], 0, h)
-            tanh_gain(z0[h][:], 0)
-        page.append(load_page(1, "C"))
-        load_wgs(wgs12, S, 2, 0, S)
-        nc.vector.tensor_tensor(out=page[0][:].indirect(list3[:, 0:32]), in0=z0[0][:], in1=wgs00[:], op=MULT)
-        page.append(load_page(2, "G"))
-        wgs3 = sb("wgs3", S + 16, F32, "E")
-        load_wgs(wgs3, 0, 3, 0, S)
-        z = [None]
-        for t in range(1, PACK):
-            z.append(sb("z%d" % t, S, F32, "IJK"[t - 1]))
-            for h in range(2):
-                times_shot(z[t][:, h * BANK : (h + 1) * BANK], t, h)
-            tanh_gain(z[t][:], t)
-            if t == 1:
-                nc.vector.tensor_tensor(out=page[0][:].indirect(list3[:, 32:64]), in0=z0[1][:],
-                                        in1=later[:, 3 * S : 3 * S + BANK], op=MULT)
-                page.append(load_page(3, "H"))
-                pick(0)
-        wgs_sb = [None, wgs12[:, 0:S], wgs12[:, S : 2 * S], wgs3[:, 0:S]]
-        for t in range(1, PACK):
-            nc.vector.tensor_tensor(out=page[t][:].indirect(list3[:]), in0=z[t][:], in1=wgs_sb[t], op=MULT)
-            if t == 1:
-                tab2_w = sb("tab2_w", T3, I32, "I")
-                nc.sync.dma_start(out=tab2_w[:], in_=words(tab2_words, 0))
-                ca_sb = wgs3[:, S : S + 8]
-                cb_sb = wgs3[:, S + 8 : S + 16]
-                with nc.allow_non_contiguous_dma(reason="one value of ca and cb for each output row"):
-                    nc.sync.dma_start(out=ca_sb, in_=ca.rearrange("(c p) -> p c", p=P))
-                    nc.sync.dma_start(out=cb_sb, in_=cb.rearrange("(c p) -> p c", p=P))
+            tanh_gain(0, slice(h * BANK, (h + 1) * BANK))
+        times_shot(1)
+        tanh_gain(1, slice(0, S))
+        put(0, 0, BANK)
+        put(0, BANK, S)
+        for t in range(PACK - 1):
+            if t + 2 < PACK:
+                times_shot(t + 2)
+                tanh_gain(t + 2, slice(0, S))
             pick(t)
+            put(t + 1, 0, S)
 
-        v2_w = [sb("v2_w%d" % h, BANK, U32) for h in range(2)]
-        x_codes = sb("x_codes", PJ, U32)
-        x_scales = sb("x_scales", PJ, U8)
-        nc.vector.tensor_copy(out=v2_w[0][:], in_=tab2_w[:].bitcast(U32).indirect(list2[:, 0:32]))
-        nc.vector.quantize_mx(out=x_codes[:].bitcast(FP8X4), scales=x_scales[:], in_=x_bf[:])
-        nc.vector.tensor_copy(out=v2_w[1][:], in_=tab2_w[:].bitcast(U32).indirect(list2[:, 32:64]))
-        for c in range(S2 // P):
+        last = PACK - 1
+        for u in range(2):
+            cols = slice(u * HALF, (u + 1) * HALF)
+            nc.vector.tensor_copy(out=picked[last][:, cols], in_=page[last][:].indirect(list4[:, 16 * u : 16 * (u + 1)]))
+            nc.scalar.activation(out=x_slots[u][:, last, :], in_=picked[last][:, cols], func=ACT.Abs)
+
+        v2_w = sb("v2_w", S2, U32, "z1")
+        x_codes = [sb("x_codes%d" % u, HALF, U32) for u in range(2)]
+        x_scales = [sb("x_scales%d" % u, HALF, U8) for u in range(2)]
+
+        def gather_v2(n):
+            nc.vector.tensor_copy(out=v2_w[:, 256 * n : 256 * (n + 1)],
+                                  in_=tab2_w[:].bitcast(U32).indirect(list2[:, 16 * n : 16 * (n + 1)]))
+
+        def quantise_x(u):
+            nc.vector.quantize_mx(out=x_codes[u][:].bitcast(FP8X4), scales=x_scales[u][:], in_=x_bf[u][:])
+
+        gather_v2(0)
+        quantise_x(0)
+        gather_v2(1)
+        quantise_x(1)
+        gather_v2(2)
+        gather_v2(3)
+        out_rows = out.rearrange("(c p) j -> p c j", p=P)
+        for n, u in ((0, 0), (1, 0), (0, 1), (1, 1), (2, 0), (2, 1), (3, 0), (3, 1)):
             e_acc = psum.tile([P, BANK], F32, name="acc")
-            nc.tensor.matmul_mx(out=e_acc[:],
-                                lhsT=v2_w[c // 4][:, P * (c % 4) : P * (c % 4 + 1)].bitcast(FP8X4),
-                                lhsT_scale=v2_s[TAB2_PLANE:P, P * c : P * (c + 1)],
-                                rhs=x_codes[:].bitcast(FP8X4), rhs_scale=x_scales[:],
-                                start=True, stop=True)
-            res = sb("res%d" % c, PJ, F32)
-            if c in (3, 5, 7):
-                nc.vector.tensor_scalar(out=res[:], in0=e_acc[:], scalar1=ca_sb[:, c : c + 1],
-                                        scalar2=cb_sb[:, c : c + 1], op0=MULT, op1=ADD)
-            else:
-                nc.scalar.activation(out=res[:], in_=e_acc[:], func=ACT.Identity,
-                                     scale=ca_sb[:, c : c + 1], bias=cb_sb[:, c : c + 1])
-            nc.sync.dma_start(out=out[P * c : P * (c + 1), :], in_=res[:])
+            res = sb("res%d_%d" % (n, u), BANK, F32)
+            for i in range(2):
+                c = 2 * n + i
+                nc.tensor.matmul_mx(out=e_acc[:, HALF * i : HALF * (i + 1)],
+                                    lhsT=v2_w[:, P * c : P * (c + 1)].bitcast(FP8X4),
+                                    lhsT_scale=v2_s[TAB2_PLANE:P, P * c : P * (c + 1)],
+                                    rhs=x_codes[u][:].bitcast(FP8X4), rhs_scale=x_scales[u][:],
+                                    start=True, stop=True)
+            for i in range(2):
+                c = 2 * n + i
+                cols = slice(HALF * i, HALF * (i + 1))
+                if (n, u) in ((1, 1), (2, 1), (3, 1)):
+                    nc.vector.tensor_scalar(out=res[:, cols], in0=e_acc[:, cols], scalar1=ca_sb[:, c : c + 1],
+                                            scalar2=cb_sb[:, c : c + 1], op0=MULT, op1=ADD)
+                else:
+                    nc.scalar.activation(out=res[:, cols], in_=e_acc[:, cols], func=ACT.Identity,
+                                         scale=ca_sb[:, c : c + 1], bias=cb_sb[:, c : c + 1])
+            nc.sync.dma_start(out=out_rows[:, 2 * n : 2 * n + 2, HALF * u : HALF * (u + 1)],
+                              in_=res[:].rearrange("p (i j) -> p i j", i=2))

@@ -1,6 +1,7 @@
 from contextlib import ExitStack
 
 import concourse.mybir as mybir
+from concourse.masks import make_identity
 
 K, KA, T, H, S, T2, PJ, S2, T3 = 1536, 1024, 4096, 512, 1024, 2048, 512, 1024, 2048
 FLOPS = 2 * K * H * S + 2 * H * S2 * PJ
@@ -50,8 +51,10 @@ def tile_list_footage_clip_storyboard_kernel(
         w4_raw_s = sb("w4_raw_s", H, U8)
         b1_sb = sb("b1_sb", PACK, F32)
         gain_sb = sb("gain_sb", PACK, F32)
-        ca_sb = sb("ca_sb", S2 // P, F32)
-        cb_sb = sb("cb_sb", S2 // P, F32)
+        cab_rows = sb("cab_rows", P, F32)
+        ident = sb("ident", P, F32)
+        cab = sb("cab", 2 * S2 // P, F32)
+        v_s = [sb("v_s%d" % a, S, U8) for a in range(3)]
         shot_sb = [sb("shot%d" % t, S, F32) for t in range(PACK)]
         wgs_sb = [sb("wgs%d" % t, S, F32) for t in range(PACK)]
         page = [sb("page%d" % t, T2, F32) for t in range(PACK)]
@@ -68,12 +71,16 @@ def tile_list_footage_clip_storyboard_kernel(
             return [(wgs_sb[t][32 * g : 32 * g + 32, lo:hi], wgs_rows[:, t, lo:hi]) for g in QUADS]
 
         def scale_loads(tile, first, scales, a):
-            return [(tile[32 * q + first : 32 * q + first + 4, :].bitcast(I32),
-                     scales.bitcast(I32)[a, 4 * q : 4 * q + 4, :]) for q in QUADS]
+            return [(tile[first + r : P : 32, :].bitcast(I32), scales.bitcast(I32)[a, r : 16 : 4, :])
+                    for r in range(4)]
 
         nc.vector.memset(tab_s[:].bitcast(I32), 0)
         nc.gpsimd.memset(tab2_s[:].bitcast(I32), 0)
         nc.gpsimd.memset(w4_raw_s[:].bitcast(I32), 0)
+        for a in range(3):
+            nc.gpsimd.memset(v_s[a][:].bitcast(I32), 0)
+        nc.gpsimd.memset(cab_rows[:], 0.0)
+        make_identity(nc, ident[:])
 
         def tab_half(a, u):
             cols = slice(u * T // 2, (u + 1) * T // 2)
@@ -82,26 +89,35 @@ def tile_list_footage_clip_storyboard_kernel(
         def w1_rows(a):
             return (w1_raw[a][:], w1[512 * a : 512 * (a + 1), :].rearrange("(p j) c -> p (j c)", j=PACK))
 
-        tab_s_loads = []
-        for a in range(3):
-            tab_s_loads.extend(scale_loads(tab_s, TAB_PLANE[a], tab_scales, a))
-        loads = [tab_half(0, 0), (list1[:], offs), (w4_raw[:].bitcast(I32), w4_words[0].bitcast(I32)), tab_half(0, 1),
+        tab_s_rows = tab_scales.bitcast(I32).rearrange("a q n -> (a q) n")
+        loads = [tab_half(0, 0), (list1[:], offs), (w4_raw[:].bitcast(I32), w4_words[0].bitcast(I32)), w1_rows(0),
                  (list2[:], offs2), (list3[:], offs3),
                  (b1_sb[:], b1.rearrange("(p t) -> p t", t=PACK)),
-                 (gain_sb[:], gain.rearrange("(p t) -> p t", t=PACK)), w1_rows(0)]
+                 (gain_sb[:], gain.rearrange("(p t) -> p t", t=PACK)),
+                 (tab_s[0:P:4, :].bitcast(I32), tab_s_rows[0:32, :]),
+                 (tab_s[1:P:8, :].bitcast(I32), tab_s_rows[32:48, :]),
+                 tab_half(0, 1)]
         loads.extend(scale_loads(tab2_s, TAB2_PLANE, tab2_scales, 0))
-        loads.extend(tab_s_loads[:2])
-        loads.append(w1_rows(1))
-        loads.extend(tab_s_loads[2:8])
-        loads.append(tab_half(1, 0))
-        loads.extend(tab_s_loads[8:])
-        loads.extend([tab_half(1, 1), tab_half(2, 0)])
+        loads.extend([w1_rows(1), tab_half(1, 0), tab_half(1, 1)])
+        for pair in loads:
+            nc.sync.dma_start(*pair)
+
+        picked_s = sb("picked_s", S, U8)
+        nc.vector.tensor_copy(out=picked_s[:], in_=tab_s[:].indirect(list1[:]))
+        moves = []
+        for a in range(3):
+            for r in range(4):
+                src = picked_s[64 * a + 4 * r : 64 * (a + 1) : 16, :] if a < 2 else picked_s[1 + 8 * r : P : 32, :]
+                moves.append((v_s[a][TAB_PLANE[a] + r : P : 32, :].bitcast(I32), src.bitcast(I32)))
+        loads = moves[:6] + [tab_half(2, 0)] + moves[6:] + [tab_half(2, 1)]
         loads.extend(scale_loads(w4_raw_s, 0, w4_scales, 0))
-        loads.extend([tab_half(2, 1), (shot_sb[0][:], shot_rows[:, 0, :]), (shot_sb[1][:], shot_rows[:, 1, :])])
+        loads.extend([(shot_sb[0][:], shot_rows[:, 0, :]), (shot_sb[1][:], shot_rows[:, 1, :])])
         loads.extend(wgs_loads(0, 0, BANK))
         loads.append((page[0][:], page_rows[:, 0, :]))
         loads.extend(wgs_loads(0, BANK, S))
         loads.append((list4[:], offs4))
+        loads.append((cab_rows[0:8, :], ca.rearrange("(c p) -> c p", p=P)))
+        loads.append((cab_rows[8:16, :], cb.rearrange("(c p) -> c p", p=P)))
         for t in range(1, PACK):
             if t + 1 < PACK:
                 loads.append((shot_sb[t + 1][:], shot_rows[:, t + 1, :]))
@@ -111,13 +127,9 @@ def tile_list_footage_clip_storyboard_kernel(
             loads.append((page[t][:], page_rows[:, t, :]))
         for pair in loads:
             nc.sync.dma_start(*pair)
-        with nc.allow_non_contiguous_dma(reason="one value of ca and cb for each output row"):
-            nc.sync.dma_start(out=ca_sb[:], in_=ca.rearrange("(c p) -> p c", p=P))
-            nc.sync.dma_start(out=cb_sb[:], in_=cb.rearrange("(c p) -> p c", p=P))
 
         v_w = [sb("v_w%d" % a, S, U32) for a in range(2)]
         v_w2 = [sb("v_w2_%d" % h, BANK, U32) for h in range(2)]
-        v_s = sb("v_s", S, U8)
         v2_s = sb("v2_s", S2, U8)
         w4_codes = sb("w4_codes", 2 * H, U8)
         w4_s = sb("w4_s", H, U8)
@@ -132,7 +144,6 @@ def tile_list_footage_clip_storyboard_kernel(
 
         nc.vector.tensor_copy(out=v_w[0][:], in_=tab_w[0][:].bitcast(U32).indirect(list1[:]))
         quantise_w1(0)
-        nc.vector.tensor_copy(out=v_s[:], in_=tab_s[:].indirect(list1[:]))
         quantise_w1(1)
         nc.vector.tensor_copy(out=v_w[1][:], in_=tab_w[1][:].bitcast(U32).indirect(list1[:]))
         for h in range(2):
@@ -158,9 +169,12 @@ def tile_list_footage_clip_storyboard_kernel(
                         lhs_s = w4_s[:, P * t : P * (t + 1)]
                         rhs = v_w2[h][:]
                     nc.tensor.matmul_mx(out=f_acc[t][h][:], lhsT=lhs, lhsT_scale=lhs_s,
-                                        rhs=rhs.bitcast(FP8X4), rhs_scale=v_s[TAB_PLANE[a] : P, cols],
+                                        rhs=rhs.bitcast(FP8X4), rhs_scale=v_s[a][TAB_PLANE[a] : P, cols],
                                         start=(a == 0), stop=(a == 2))
 
+        turned = psum.tile([P, BANK], F32, name="acc")
+        nc.tensor.transpose(turned[:, 0:P], cab_rows[:], ident[:])
+        nc.scalar.copy(out=cab[:], in_=turned[:, 0 : 2 * S2 // P])
         HALF = PJ // 2
         x_bf = [sb("x_bf%d" % u, PACK * HALF, BF16) for u in range(2)]
         x_slots = [x_bf[u][:].rearrange("p (j t) -> p t j", t=PACK) for u in range(2)]
@@ -239,10 +253,10 @@ def tile_list_footage_clip_storyboard_kernel(
                 c = 2 * n + i
                 cols = slice(HALF * i, HALF * (i + 1))
                 if (n, u) in ((1, 1), (2, 1), (3, 1)):
-                    nc.vector.tensor_scalar(out=res[:, cols], in0=e_acc[:, cols], scalar1=ca_sb[:, c : c + 1],
-                                            scalar2=cb_sb[:, c : c + 1], op0=MULT, op1=ADD)
+                    nc.vector.tensor_scalar(out=res[:, cols], in0=e_acc[:, cols], scalar1=cab[:, c : c + 1],
+                                            scalar2=cab[:, 8 + c : 9 + c], op0=MULT, op1=ADD)
                 else:
                     nc.scalar.activation(out=res[:, cols], in_=e_acc[:, cols], func=ACT.Identity,
-                                         scale=ca_sb[:, c : c + 1], bias=cb_sb[:, c : c + 1])
+                                         scale=cab[:, c : c + 1], bias=cab[:, 8 + c : 9 + c])
             nc.sync.dma_start(out=out_rows[:, 2 * n : 2 * n + 2, HALF * u : HALF * (u + 1)],
                               in_=res[:].rearrange("p (i j) -> p i j", i=2))

@@ -98,7 +98,9 @@ def tile_list_footage_clip_storyboard_kernel(
                  (tab_s[1:P:8, :].bitcast(I32), tab_s_rows[32:48, :]),
                  tab_half(0, 1)]
         loads.extend(scale_loads(tab2_s, TAB2_PLANE, tab2_scales, 0))
-        loads.extend([w1_rows(1), tab_half(1, 0), tab_half(1, 1)])
+        loads.extend([w1_rows(1), tab_half(1, 0)])
+        loads.extend(scale_loads(w4_raw_s, 0, w4_scales, 0))
+        loads.append(tab_half(1, 1))
         for pair in loads:
             nc.sync.dma_start(*pair)
 
@@ -110,18 +112,16 @@ def tile_list_footage_clip_storyboard_kernel(
                 src = picked_s[64 * a + 4 * r : 64 * (a + 1) : 16, :] if a < 2 else picked_s[1 + 8 * r : P : 32, :]
                 moves.append((v_s[a][TAB_PLANE[a] + r : P : 32, :].bitcast(I32), src.bitcast(I32)))
         loads = moves[:6] + [tab_half(2, 0)] + moves[6:] + [tab_half(2, 1)]
-        loads.extend(scale_loads(w4_raw_s, 0, w4_scales, 0))
         loads.extend([(shot_sb[0][:], shot_rows[:, 0, :]), (shot_sb[1][:], shot_rows[:, 1, :])])
         loads.extend(wgs_loads(0, 0, BANK))
         loads.append((page[0][:], page_rows[:, 0, :]))
+        loads.extend((shot_sb[t][:], shot_rows[:, t, :]) for t in (2, 3))
         loads.extend(wgs_loads(0, BANK, S))
         loads.append((list4[:], offs4))
         loads.append((cab_rows[0:8, :], ca.rearrange("(c p) -> c p", p=P)))
         loads.append((cab_rows[8:16, :], cb.rearrange("(c p) -> c p", p=P)))
         for t in range(1, PACK):
-            if t + 1 < PACK:
-                loads.append((shot_sb[t + 1][:], shot_rows[:, t + 1, :]))
-            else:
+            if t == PACK - 1:
                 loads.append((tab2_w[:], words(tab2_words, 0)))
             loads.extend(wgs_loads(t, 0, S))
             loads.append((page[t][:], page_rows[:, t, :]))
@@ -149,10 +149,10 @@ def tile_list_footage_clip_storyboard_kernel(
         for h in range(2):
             nc.vector.tensor_copy(out=v_w2[h][:],
                                   in_=tab_w[2][:].bitcast(U32).indirect(list1[:, 32 * h : 32 * (h + 1)]))
-        nc.vector.tensor_copy(out=w4_codes[:].rearrange("p (t m b) -> p m t b", t=PACK, b=2),
-                              in_=w4_raw[:].rearrange("p (m t b) -> p m t b", t=PACK, b=2))
-        nc.vector.tensor_copy(out=w4_s[:].rearrange("p (t m) -> p m t", t=PACK),
-                              in_=w4_raw_s[:].rearrange("p (m t) -> p m t", t=PACK))
+        nc.vector.tensor_copy(out=w4_codes[:].rearrange("p (t m b) -> p t m b", t=PACK, b=2),
+                              in_=w4_raw[:].rearrange("p (m t b) -> p t m b", t=PACK, b=2))
+        nc.vector.tensor_copy(out=w4_s[:].rearrange("p (t m) -> p t m", t=PACK),
+                              in_=w4_raw_s[:].rearrange("p (m t) -> p t m", t=PACK))
         nc.vector.tensor_copy(out=v2_s[:], in_=tab2_s[:].indirect(list2[:]))
 
         f_acc = [[psum.tile([P, BANK], F32, name="acc") for h in range(2)] for t in range(PACK)]
@@ -178,59 +178,56 @@ def tile_list_footage_clip_storyboard_kernel(
         HALF = PJ // 2
         x_bf = [sb("x_bf%d" % u, PACK * HALF, BF16) for u in range(2)]
         x_slots = [x_bf[u][:].rearrange("p (j t) -> p t j", t=PACK) for u in range(2)]
-        z = {}
 
-        def times_shot(t):
-            z[t] = sb("z%d" % t, S, F32, "z%d" % (t % 2))
-            for h in range(2):
-                cols = slice(h * BANK, (h + 1) * BANK)
-                nc.vector.tensor_tensor(out=z[t][:, cols], in0=f_acc[t][h][:], in1=shot_sb[t][:, cols], op=MULT)
+        def make_h(t, lo, hi, slot):
+            z = sb("h%d_%d" % (t, lo), hi - lo, F32, slot)
+            for c in range(lo, hi, BANK):
+                nc.vector.tensor_tensor(out=z[:, c - lo : c - lo + BANK], in0=f_acc[t][c // BANK][:],
+                                        in1=shot_sb[t][:, c : c + BANK], op=MULT)
+            nc.scalar.activation(out=z[:], in_=z[:], func=ACT.Tanh, bias=b1_sb[:, t : t + 1])
+            nc.scalar.activation(out=z[:], in_=z[:], func=ACT.Copy, scale=gain_sb[:, t : t + 1])
+            return z
 
-        def tanh_gain(t, cols):
-            nc.scalar.activation(out=z[t][:, cols], in_=z[t][:, cols], func=ACT.Tanh, bias=b1_sb[:, t : t + 1])
-            nc.scalar.activation(out=z[t][:, cols], in_=z[t][:, cols], func=ACT.Copy, scale=gain_sb[:, t : t + 1])
-
-        def put(t, lo, hi):
+        def put(t, lo, hi, z):
             nc.vector.tensor_tensor(out=page[t][:].indirect(list3[:, lo // 16 : hi // 16]),
-                                    in0=z[t][:, lo:hi], in1=wgs_sb[t][:, lo:hi], op=MULT)
+                                    in0=z[:], in1=wgs_sb[t][:, lo:hi], op=MULT)
 
-        picked = [sb("picked%d" % t, PJ, F32) for t in range(PACK)]
+        def pick(t, lo, hi, slot):
+            picked = sb("picked%d_%d" % (t, lo), hi - lo, F32, slot)
+            nc.vector.tensor_copy(out=picked[:], in_=page[t][:].indirect(list4[:, lo // 16 : hi // 16]))
+            for c in range(lo, hi, HALF):
+                nc.scalar.activation(out=x_slots[c // HALF][:, t, :], in_=picked[:, c - lo : c - lo + HALF], func=ACT.Abs)
+            return picked
 
-        def pick(t):
-            nc.vector.tensor_copy(out=picked[t][:], in_=page[t][:].indirect(list4[:]))
-            for u in range(2):
-                nc.scalar.activation(out=x_slots[u][:, t, :], in_=picked[t][:, u * HALF : (u + 1) * HALF], func=ACT.Abs)
+        h0a = make_h(0, 0, BANK, "left")
+        h0b = make_h(0, BANK, S, "right")
+        h1 = make_h(1, 0, S, "h1")
+        put(0, 0, BANK, h0a)
+        h2 = make_h(2, 0, S, "h2")
+        h3a = make_h(3, 0, BANK, "left")
+        put(0, BANK, S, h0b)
+        h3b = make_h(3, BANK, S, "right")
+        pick(0, 0, PJ, None)
+        put(1, 0, S, h1)
+        put(2, 0, S, h2)
+        pick(1, 0, PJ, "h2")
+        put(3, 0, BANK, h3a)
+        pick(2, 0, PJ, "left")
+        put(3, BANK, S, h3b)
+        p3 = pick(3, 0, HALF, None)
+        pick(3, HALF, PJ, None)
 
-        times_shot(0)
-        for h in range(2):
-            tanh_gain(0, slice(h * BANK, (h + 1) * BANK))
-        times_shot(1)
-        tanh_gain(1, slice(0, S))
-        put(0, 0, BANK)
-        put(0, BANK, S)
-        for t in range(PACK - 1):
-            if t + 2 < PACK:
-                times_shot(t + 2)
-                tanh_gain(t + 2, slice(0, S))
-            pick(t)
-            put(t + 1, 0, S)
-
-        last = PACK - 1
-        for u in range(2):
-            cols = slice(u * HALF, (u + 1) * HALF)
-            nc.vector.tensor_copy(out=picked[last][:, cols], in_=page[last][:].indirect(list4[:, 16 * u : 16 * (u + 1)]))
-            nc.scalar.activation(out=x_slots[u][:, last, :], in_=picked[last][:, cols], func=ACT.Abs)
-
-        v2_w = sb("v2_w", S2, U32, "z1")
-        x_codes = [sb("x_codes%d" % u, HALF, U32) for u in range(2)]
-        x_scales = [sb("x_scales%d" % u, HALF, U8) for u in range(2)]
+        v2_w = sb("v2_w", S2, U32, "right")
+        x_codes = sb("x_codes", PJ, U32)
+        x_scales = sb("x_scales", PJ, U8)
 
         def gather_v2(n):
             nc.vector.tensor_copy(out=v2_w[:, 256 * n : 256 * (n + 1)],
                                   in_=tab2_w[:].bitcast(U32).indirect(list2[:, 16 * n : 16 * (n + 1)]))
 
         def quantise_x(u):
-            nc.vector.quantize_mx(out=x_codes[u][:].bitcast(FP8X4), scales=x_scales[u][:], in_=x_bf[u][:])
+            cols = slice(HALF * u, HALF * (u + 1))
+            nc.vector.quantize_mx(out=x_codes[:, cols].bitcast(FP8X4), scales=x_scales[:, cols], in_=x_bf[u][:])
 
         gather_v2(0)
         quantise_x(0)
@@ -239,24 +236,29 @@ def tile_list_footage_clip_storyboard_kernel(
         gather_v2(2)
         gather_v2(3)
         out_rows = out.rearrange("(c p) j -> p c j", p=P)
-        for n, u in ((0, 0), (1, 0), (0, 1), (1, 1), (2, 0), (2, 1), (3, 0), (3, 1)):
+
+        def scores(blocks, lo, hi, on_vector):
+            width = hi - lo
             e_acc = psum.tile([P, BANK], F32, name="acc")
-            res = sb("res%d_%d" % (n, u), BANK, F32)
-            for i in range(2):
-                c = 2 * n + i
-                nc.tensor.matmul_mx(out=e_acc[:, HALF * i : HALF * (i + 1)],
+            res = sb("res%d_%d" % (blocks[0], lo), BANK, F32)
+            for i, c in enumerate(blocks):
+                nc.tensor.matmul_mx(out=e_acc[:, width * i : width * (i + 1)],
                                     lhsT=v2_w[:, P * c : P * (c + 1)].bitcast(FP8X4),
                                     lhsT_scale=v2_s[TAB2_PLANE:P, P * c : P * (c + 1)],
-                                    rhs=x_codes[u][:].bitcast(FP8X4), rhs_scale=x_scales[u][:],
+                                    rhs=x_codes[:, lo:hi].bitcast(FP8X4), rhs_scale=x_scales[:, lo:hi],
                                     start=True, stop=True)
-            for i in range(2):
-                c = 2 * n + i
-                cols = slice(HALF * i, HALF * (i + 1))
-                if (n, u) in ((1, 1), (2, 1), (3, 1)):
+            for i, c in enumerate(blocks):
+                cols = slice(width * i, width * (i + 1))
+                if on_vector:
                     nc.vector.tensor_scalar(out=res[:, cols], in0=e_acc[:, cols], scalar1=cab[:, c : c + 1],
                                             scalar2=cab[:, 8 + c : 9 + c], op0=MULT, op1=ADD)
                 else:
                     nc.scalar.activation(out=res[:, cols], in_=e_acc[:, cols], func=ACT.Identity,
                                          scale=cab[:, c : c + 1], bias=cab[:, 8 + c : 9 + c])
-            nc.sync.dma_start(out=out_rows[:, 2 * n : 2 * n + 2, HALF * u : HALF * (u + 1)],
-                              in_=res[:].rearrange("p (i j) -> p i j", i=2))
+            nc.sync.dma_start(out=out_rows[:, blocks[0] : blocks[-1] + 1, lo:hi],
+                              in_=res[:].rearrange("p (i j) -> p i j", i=len(blocks)))
+
+        scores((0, 1), 0, HALF, False)
+        for c in range(2, S2 // P):
+            scores((c,), 0, PJ, c in (5, 7))
+        scores((0, 1), HALF, PJ, False)

from contextlib import ExitStack

import concourse.mybir as mybir
from concourse.masks import make_identity

K, KA, T, H, S, T2, PJ, S2, T3 = 1536, 1024, 4096, 512, 1024, 2048, 512, 1024, 2048
FLOPS = 2 * K * H * S + 2 * H * S2 * PJ

F32 = mybir.dt.float32
BF16 = mybir.dt.bfloat16
I32 = mybir.dt.int32
U32 = mybir.dt.uint32
U16 = mybir.dt.uint16
U8 = mybir.dt.uint8
FP8X4 = mybir.dt.float8_e4m3fn_x4
FP4X4 = mybir.dt.float4_e2m1fn_x4
ACT = mybir.ActivationFunctionType
MULT = mybir.AluOpType.mult
ADD = mybir.AluOpType.add

P = 128
PACK = 4
BANK = 512
TAB_PLANE = (4, 8, 0)
TAB2_PLANE = 12
QUADS = (0, 2, 1, 3)


def tile_list_footage_clip_storyboard_kernel(
    tc, tab_words, tab_scales, tab2_words, tab2_scales, w1, w4_words, w4_scales,
    shot, b1, gain, page0, wgs, ca, cb, offs, offs2, offs3, offs4, out,
):
    nc = tc.nc
    with ExitStack() as ctx:
        keep = ctx.enter_context(tc.tile_pool(name="keep", bufs=1))
        psum = ctx.enter_context(tc.psum_pool(name="psum", bufs=8))

        def sb(name, width, dtype, slot=None):
            return keep.tile([P, width], dtype, name=name, tag=slot or name, align_bytes=64)

        list1 = keep.tile([P, S // 16], U16, name="list1")
        list2 = keep.tile([P, S2 // 16], U16, name="list2")
        list3 = keep.tile([P, S // 16], U16, name="list3")
        list4 = keep.tile([P, PJ // 16], U16, name="list4")

        tab_w = [sb("tab_w%d" % a, T, I32) for a in range(3)]
        tab_s = sb("tab_s", T, U8)
        tab2_s = sb("tab2_s", T3, U8)
        w1_raw = [sb("w1_raw%d" % a, PACK * H, F32) for a in range(2)]
        w4_raw = sb("w4_raw", 2 * H, U8)
        w4_raw_s = sb("w4_raw_s", H, U8)
        b1_sb = sb("b1_sb", PACK, F32)
        gain_sb = sb("gain_sb", PACK, F32)
        cab_rows = sb("cab_rows", P, F32)
        ident = sb("ident", P, F32)
        cab = sb("cab", 2 * S2 // P, F32)
        v_s = [sb("v_s%d" % a, S, U8) for a in range(3)]
        shot_sb = [sb("shot%d" % t, S, F32) for t in range(PACK)]
        wgs_sb = [sb("wgs%d" % t, S, F32) for t in range(PACK)]
        page = [sb("page%d" % t, T2, F32) for t in range(PACK)]
        tab2_w = sb("tab2_w", T3, I32)

        def words(table, a):
            return table[a].rearrange("p t i -> p (t i)").bitcast(I32)

        shot_rows = shot.rearrange("(p t) j -> p t j", t=PACK)
        page_rows = page0.rearrange("(p t) j -> p t j", t=PACK)
        wgs_rows = wgs.rearrange("(q t) j -> q t j", t=PACK)

        def wgs_loads(t, lo, hi):
            return [(wgs_sb[t][32 * g : 32 * g + 32, lo:hi], wgs_rows[:, t, lo:hi]) for g in QUADS]

        def scale_loads(tile, first, scales, a):
            return [(tile[first + r : P : 32, :].bitcast(I32), scales.bitcast(I32)[a, r : 16 : 4, :])
                    for r in range(4)]

        nc.vector.memset(tab_s[:].bitcast(I32), 0)
        nc.gpsimd.memset(tab2_s[:].bitcast(I32), 0)
        nc.gpsimd.memset(w4_raw_s[:].bitcast(I32), 0)
        for a in range(3):
            nc.gpsimd.memset(v_s[a][:].bitcast(I32), 0)
        nc.gpsimd.memset(cab_rows[:], 0.0)
        make_identity(nc, ident[:])

        def tab_half(a, u):
            cols = slice(u * T // 2, (u + 1) * T // 2)
            return (tab_w[a][:, cols], words(tab_words, a)[:, cols])

        def w1_rows(a):
            return (w1_raw[a][:], w1[512 * a : 512 * (a + 1), :].rearrange("(p j) c -> p (j c)", j=PACK))

        tab_s_rows = tab_scales.bitcast(I32).rearrange("a q n -> (a q) n")
        loads = [tab_half(0, 0), (list1[:], offs), (w4_raw[:].bitcast(I32), w4_words[0].bitcast(I32)), w1_rows(0),
                 (list2[:], offs2), (list3[:], offs3),
                 (b1_sb[:], b1.rearrange("(p t) -> p t", t=PACK)),
                 (gain_sb[:], gain.rearrange("(p t) -> p t", t=PACK)),
                 (tab_s[0:P:4, :].bitcast(I32), tab_s_rows[0:32, :]),
                 (tab_s[1:P:8, :].bitcast(I32), tab_s_rows[32:48, :]),
                 tab_half(0, 1)]
        loads.extend(scale_loads(tab2_s, TAB2_PLANE, tab2_scales, 0))
        loads.extend([w1_rows(1), tab_half(1, 0)])
        loads.extend(scale_loads(w4_raw_s, 0, w4_scales, 0))
        loads.append(tab_half(1, 1))
        for pair in loads:
            nc.sync.dma_start(*pair)

        picked_s = sb("picked_s", S, U8)
        nc.vector.tensor_copy(out=picked_s[:], in_=tab_s[:].indirect(list1[:]))
        moves = []
        for a in range(3):
            for r in range(4):
                src = picked_s[64 * a + 4 * r : 64 * (a + 1) : 16, :] if a < 2 else picked_s[1 + 8 * r : P : 32, :]
                moves.append((v_s[a][TAB_PLANE[a] + r : P : 32, :].bitcast(I32), src.bitcast(I32)))
        loads = moves[:6] + [tab_half(2, 0)] + moves[6:] + [tab_half(2, 1)]
        loads.extend([(shot_sb[0][:], shot_rows[:, 0, :]), (shot_sb[1][:], shot_rows[:, 1, :])])
        loads.extend(wgs_loads(0, 0, BANK))
        loads.append((page[0][:], page_rows[:, 0, :]))
        loads.extend((shot_sb[t][:], shot_rows[:, t, :]) for t in (2, 3))
        loads.extend(wgs_loads(0, BANK, S))
        loads.append((list4[:], offs4))
        loads.append((cab_rows[0:8, :], ca.rearrange("(c p) -> c p", p=P)))
        loads.append((cab_rows[8:16, :], cb.rearrange("(c p) -> c p", p=P)))
        for t in range(1, PACK):
            if t == PACK - 1:
                loads.append((tab2_w[:], words(tab2_words, 0)))
            loads.extend(wgs_loads(t, 0, S))
            loads.append((page[t][:], page_rows[:, t, :]))
        for pair in loads:
            nc.sync.dma_start(*pair)

        v_w = [sb("v_w%d" % a, S, U32) for a in range(2)]
        v_w2 = [sb("v_w2_%d" % h, BANK, U32) for h in range(2)]
        v2_s = sb("v2_s", S2, U8)
        w4_codes = sb("w4_codes", 2 * H, U8)
        w4_s = sb("w4_s", H, U8)
        w1_codes = [sb("w1_codes%d" % a, H, U32) for a in range(2)]
        w1_scales = [sb("w1_scales%d" % a, H, U8) for a in range(2)]

        def quantise_w1(a):
            rounded = sb("w1_bf%d" % a, PACK * H, BF16)
            nc.scalar.copy(out=rounded[:].rearrange("p (t m j) -> p m t j", t=PACK, j=PACK),
                           in_=w1_raw[a][:].rearrange("p (j m t) -> p m t j", j=PACK, t=PACK))
            nc.vector.quantize_mx(out=w1_codes[a][:].bitcast(FP8X4), scales=w1_scales[a][:], in_=rounded[:])

        nc.vector.tensor_copy(out=v_w[0][:], in_=tab_w[0][:].bitcast(U32).indirect(list1[:]))
        quantise_w1(0)
        quantise_w1(1)
        nc.vector.tensor_copy(out=v_w[1][:], in_=tab_w[1][:].bitcast(U32).indirect(list1[:]))
        for h in range(2):
            nc.vector.tensor_copy(out=v_w2[h][:],
                                  in_=tab_w[2][:].bitcast(U32).indirect(list1[:, 32 * h : 32 * (h + 1)]))
        nc.vector.tensor_copy(out=w4_codes[:].rearrange("p (t m b) -> p t m b", t=PACK, b=2),
                              in_=w4_raw[:].rearrange("p (m t b) -> p t m b", t=PACK, b=2))
        nc.vector.tensor_copy(out=w4_s[:].rearrange("p (t m) -> p t m", t=PACK),
                              in_=w4_raw_s[:].rearrange("p (m t) -> p t m", t=PACK))
        nc.vector.tensor_copy(out=v2_s[:], in_=tab2_s[:].indirect(list2[:]))

        f_acc = [[psum.tile([P, BANK], F32, name="acc") for h in range(2)] for t in range(PACK)]
        for t in range(PACK):
            for h in range(2):
                for a in range(3):
                    cols = slice(h * BANK, (h + 1) * BANK)
                    if a < 2:
                        lhs = w1_codes[a][:, P * t : P * (t + 1)].bitcast(FP8X4)
                        lhs_s = w1_scales[a][:, P * t : P * (t + 1)]
                        rhs = v_w[a][:, cols]
                    else:
                        lhs = w4_codes[:, 2 * P * t : 2 * P * (t + 1)].bitcast(FP4X4)
                        lhs_s = w4_s[:, P * t : P * (t + 1)]
                        rhs = v_w2[h][:]
                    nc.tensor.matmul_mx(out=f_acc[t][h][:], lhsT=lhs, lhsT_scale=lhs_s,
                                        rhs=rhs.bitcast(FP8X4), rhs_scale=v_s[a][TAB_PLANE[a] : P, cols],
                                        start=(a == 0), stop=(a == 2))

        turned = psum.tile([P, BANK], F32, name="acc")
        nc.tensor.transpose(turned[:, 0:P], cab_rows[:], ident[:])
        nc.scalar.copy(out=cab[:], in_=turned[:, 0 : 2 * S2 // P])
        HALF = PJ // 2
        x_bf = [sb("x_bf%d" % u, PACK * HALF, BF16) for u in range(2)]
        x_slots = [x_bf[u][:].rearrange("p (j t) -> p t j", t=PACK) for u in range(2)]

        def make_h(t, lo, hi, slot):
            z = sb("h%d_%d" % (t, lo), hi - lo, F32, slot)
            for c in range(lo, hi, BANK):
                nc.vector.tensor_tensor(out=z[:, c - lo : c - lo + BANK], in0=f_acc[t][c // BANK][:],
                                        in1=shot_sb[t][:, c : c + BANK], op=MULT)
            nc.scalar.activation(out=z[:], in_=z[:], func=ACT.Tanh, bias=b1_sb[:, t : t + 1])
            nc.scalar.activation(out=z[:], in_=z[:], func=ACT.Copy, scale=gain_sb[:, t : t + 1])
            return z

        def put(t, lo, hi, z):
            nc.vector.tensor_tensor(out=page[t][:].indirect(list3[:, lo // 16 : hi // 16]),
                                    in0=z[:], in1=wgs_sb[t][:, lo:hi], op=MULT)

        def pick(t, lo, hi, slot):
            picked = sb("picked%d_%d" % (t, lo), hi - lo, F32, slot)
            nc.vector.tensor_copy(out=picked[:], in_=page[t][:].indirect(list4[:, lo // 16 : hi // 16]))
            for c in range(lo, hi, HALF):
                nc.scalar.activation(out=x_slots[c // HALF][:, t, :], in_=picked[:, c - lo : c - lo + HALF], func=ACT.Abs)
            return picked

        h0a = make_h(0, 0, BANK, "left")
        h0b = make_h(0, BANK, S, "right")
        h1 = make_h(1, 0, S, "h1")
        put(0, 0, BANK, h0a)
        h2 = make_h(2, 0, S, "h2")
        h3a = make_h(3, 0, BANK, "left")
        put(0, BANK, S, h0b)
        h3b = make_h(3, BANK, S, "right")
        pick(0, 0, PJ, None)
        put(1, 0, S, h1)
        put(2, 0, S, h2)
        pick(1, 0, PJ, "h2")
        put(3, 0, BANK, h3a)
        pick(2, 0, PJ, "left")
        put(3, BANK, S, h3b)
        p3 = pick(3, 0, HALF, None)
        pick(3, HALF, PJ, None)

        v2_w = sb("v2_w", S2, U32, "right")
        x_codes = sb("x_codes", PJ, U32)
        x_scales = sb("x_scales", PJ, U8)

        def gather_v2(n):
            nc.vector.tensor_copy(out=v2_w[:, 256 * n : 256 * (n + 1)],
                                  in_=tab2_w[:].bitcast(U32).indirect(list2[:, 16 * n : 16 * (n + 1)]))

        def quantise_x(u):
            cols = slice(HALF * u, HALF * (u + 1))
            nc.vector.quantize_mx(out=x_codes[:, cols].bitcast(FP8X4), scales=x_scales[:, cols], in_=x_bf[u][:])

        gather_v2(0)
        quantise_x(0)
        gather_v2(1)
        quantise_x(1)
        gather_v2(2)
        gather_v2(3)
        out_rows = out.rearrange("(c p) j -> p c j", p=P)

        def scores(blocks, lo, hi, on_vector):
            width = hi - lo
            e_acc = psum.tile([P, BANK], F32, name="acc")
            res = sb("res%d_%d" % (blocks[0], lo), BANK, F32)
            for i, c in enumerate(blocks):
                nc.tensor.matmul_mx(out=e_acc[:, width * i : width * (i + 1)],
                                    lhsT=v2_w[:, P * c : P * (c + 1)].bitcast(FP8X4),
                                    lhsT_scale=v2_s[TAB2_PLANE:P, P * c : P * (c + 1)],
                                    rhs=x_codes[:, lo:hi].bitcast(FP8X4), rhs_scale=x_scales[:, lo:hi],
                                    start=True, stop=True)
            for i, c in enumerate(blocks):
                cols = slice(width * i, width * (i + 1))
                if on_vector:
                    nc.vector.tensor_scalar(out=res[:, cols], in0=e_acc[:, cols], scalar1=cab[:, c : c + 1],
                                            scalar2=cab[:, 8 + c : 9 + c], op0=MULT, op1=ADD)
                else:
                    nc.scalar.activation(out=res[:, cols], in_=e_acc[:, cols], func=ACT.Identity,
                                         scale=cab[:, c : c + 1], bias=cab[:, 8 + c : 9 + c])
            nc.sync.dma_start(out=out_rows[:, blocks[0] : blocks[-1] + 1, lo:hi],
                              in_=res[:].rearrange("p (i j) -> p i j", i=len(blocks)))

        scores((0, 1), 0, HALF, False)
        for c in range(2, S2 // P):
            scores((c,), 0, PJ, c in (5, 7))
        scores((0, 1), HALF, PJ, False)
